import numpy as np, ml_dtypes
CORES = [16,17,18,19,32,33,34,35]
N = 8
import mx_ref
BF = ml_dtypes.bfloat16
def gentries(a):
    return np.ascontiguousarray(a.reshape(8, 16, -1).transpose(0, 2, 1)).reshape(8, -1)
def gtable(e):
    e = np.asarray(e); return np.ascontiguousarray(e.reshape(8, -1, 16).transpose(0, 2, 1)).reshape(128, -1).astype(np.int32)
def gcols(t, e):
    v = np.concatenate([t.reshape(8, 16, -1, 4), np.zeros((8, 16, 1, 4), BF)], axis=2)
    return np.ascontiguousarray(np.stack([v[g][:, e[g]] for g in range(8)])).reshape(128, -1)
def tile(rs):
    return np.stack(rs, axis=2).reshape(128, -1).astype(BF)
def cut(t, i, w=512):
    return t[:, w * i:w * i + w]
def pick(q, e):
    c = np.concatenate([q[0].reshape(128, -1, 4), np.zeros((128, 1, 4), np.uint8)], axis=1); s = np.concatenate([q[1], np.ones((16, 1), np.uint8)], axis=1)
    return (np.ascontiguousarray(c[:, e].reshape(128, -1)), np.ascontiguousarray(s[:, e]))
def join(*qs):
    return (np.concatenate([q[0] for q in qs], axis=1), np.concatenate([q[1] for q in qs], axis=1))
def put(q, e, v):
    c, s = q[0].reshape(128, -1, 4).copy(), q[1].copy(); c[:, e] = v[0].reshape(128, -1, 4); s[:, e] = v[1]
    return (c.reshape(128, -1), s)
def pk(c, s):
    return (np.ascontiguousarray(c), mx_ref.live(s))
def emit(q):
    return q[0], q[1]
def packed(v, rng):
    q = [mx_ref.quantize(np.ascontiguousarray(v[r])) for r in range(N)]
    return np.stack([a for a, b in q]), np.stack([mx_ref.plane(b, rng) for a, b in q])
def values_of_codes():
    e, c = np.zeros((128, 128, 4), np.float32), np.zeros((128, 2, 4), np.uint8)
    e[np.arange(128), np.arange(128), 0] = 1
    c[:127, :, 0] = np.arange(256).reshape(2, 128).T[:127]
    return mx_ref.matmul(mx_ref.quantize(e.reshape(128, 512).astype(BF)), (c.reshape(128, 8), np.full((16, 2), 127, np.uint8))).T.reshape(-1).astype(np.float64)
CODE_VALUE, SCALE_VALUE = values_of_codes(), 2.0 ** (np.arange(256) - 127.0)
def decode(q):
    return (CODE_VALUE[q[0]].reshape(16, 8, -1, 4) * SCALE_VALUE[q[1]][:, None, :, None] + 0.0).reshape(128, -1).astype(np.float32)
def f(rng, *shape):
    return mx_ref.flush((rng.standard_normal(shape, dtype=np.float32) * np.exp2(rng.integers(-2, 3, shape[:-1] + (1,)))).astype(BF))
def wide(rng, *shape, cols=0):
    v = rng.standard_normal(shape, dtype=np.float32) * np.exp2(rng.integers(-12, 13, shape)).astype(np.float32)
    if cols: v *= np.repeat(np.exp2(rng.integers(-cols, cols + 1, shape[:-2] + (1, shape[-1] // 4))) * (rng.random(shape[:-2] + (1, shape[-1] // 4)) > 0.0625), 4, axis=-1).astype(np.float32)
    return mx_ref.flush(v.astype(BF))
C, G, R, L = 448, 256, 3, 3
def big(v, k):
    v = v.astype(np.float32) * np.float32(k)
    v[np.abs(v) < np.float32(2.0 ** -16)] = 0
    return v.astype(BF)
def numbers_of(rng):
    return {"x": big(f(rng, N, 128, 4 * C), 1), "gh": big(f(rng, N, 128, 4 * G), 1), "u": np.array(f(rng, N, 128, 512)), "v": np.array(f(rng, N, 128, 512))}
def weights(rng, w):
    c, p = packed(np.stack([w] * N), rng)
    return {"wc": c, "ws": p}
def still(rng):
    w = np.zeros((128, 4, 128, 4), np.float32)
    i = np.arange(128)
    for b in range(4): w[i, b, i, b] = 32
    return weights(rng, w.reshape(128, 2048).astype(BF))
def matching(rng, n):
    p, i = np.arange(C), rng.permutation(C)[:n]
    h = n // 2
    p[i[:h]] = i[h:2 * h]
    p[i[h:2 * h]] = i[:h]
    return p
def stored(nx, pr):
    return {"nx": np.stack([gtable(nx[r]) for r in range(N)]), "pr": np.stack([gtable(pr[r].reshape(8, R * C)) for r in range(N)])}
def lists_of(rng, same=(), halves=()):
    nx = rng.permuted(np.tile(np.arange(C + G), (N, 8, 1)), axis=2)
    for r in same: nx[r] = nx[r, 0].copy()
    pr = np.stack([matching(rng, C) for i in range(N * 8 * R)]).reshape(N, 8, R, C)
    h = C // 2
    for r in halves:
        for g in range(8):
            for lo, hi in ((0, h), (h, C), (C, C + G)): nx[r, g, lo:hi] = lo + rng.permutation(hi - lo)
            i = h + rng.permutation(h)
            pr[r, g, 0, :h] = i
            pr[r, g, 0, i] = np.arange(h)
    return stored(nx, pr)
def signs(rng):
    return np.stack([rng.permutation(8) % 2 * 2.0 - 1.0 for r in range(N)])
def linked(rng, kind):
    i, a, b, n = rng.permutation(C + G), rng.permutation(C), C + rng.permutation(G), np.arange(C + G)
    if kind == 1: n[i] = np.roll(i, -1)
    if kind == 2:
        n[a] = np.roll(a, -1)
        n[b] = np.roll(b, -1)
    if kind == 3:
        i = np.concatenate([np.stack([a[:G], b], axis=1).reshape(-1), a[G:]])
        n[i] = np.roll(i, -1)
    if kind == 4:
        n[i[::2]] = i[1::2]
        n[i[1::2]] = i[::2]
    if kind == 5: n = np.roll(n, -1)
    if kind == 6: n = np.roll(n, 1)
    if kind == 7: n = i
    return n
def setup_inputs(rng):
    return {**numbers_of(rng), **lists_of(rng), **weights(rng, f(rng, 128, 2048))}
def setup_inputs_ties(rng):
    d = numbers_of(rng)
    c = big(f(rng, 128, 4), 1).astype(np.float32).reshape(8, 16, 4)[:, :8]
    k = np.stack([rng.permutation(C + G) % 2 for r in range(N)])
    k[rng.integers(N)] = 1
    a = np.where(k[:, None, None, :, None] == 1, c[None, :, :, None, :], np.float32(0.0)).astype(BF)
    d["x"].reshape(N, 8, 16, C, 4)[:, :, :8] = a[:, :, :, :C]
    d["gh"].reshape(N, 8, 16, G, 4)[:, :, :8] = a[:, :, :, C:]
    keep = np.zeros((8, 16, 8), bool)
    for g in range(8): keep[g, :8, g] = True
    u = d["u"].reshape(N, 8, 16, 128, 4)
    a = u[:, :, :, ::16].astype(np.float32)
    a[:, ~keep] = 0
    u[:, :, :, ::16] = a.astype(BF)
    w = np.array(f(rng, 128, 2048)).reshape(8, 16, 4, 8, 16, 4)
    w[:, 8:, :, :, :8] = 0
    for g in range(8):
        for h in range(8):
            if g != h: w[h, :, :, g, :8] = 0
    return {**d, **lists_of(rng), **weights(rng, w.reshape(128, 2048))}
def setup_inputs_near(rng):
    d = numbers_of(rng)
    m = np.stack([rng.permutation(8) + 1 for r in range(N)])
    s = rng.integers(0, 2 ** m[:, :, None], (N, 8, C + G))
    sg, o = signs(rng), rng.permutation(N)
    full = int(np.flatnonzero(o == 3)[0])
    h = 2 ** (m[full][:, None] - 1)
    s[full] = s[full] % h + h * ((np.arange(C + G) >= C // 2)[None, :] == (sg[full] > 0)[:, None])
    g = ((s[..., None] >> np.arange(8)) & 1) * np.exp2(np.arange(8) - 23.0)
    a = np.abs(np.concatenate([d["x"], d["gh"]], axis=2).astype(np.float32)).reshape(N, 8, 16, C + G, 4)
    a[:, :, 0] = 0
    a[:, :, 0, :, 0] = 0.5
    a[:, :, 8] = g[..., :4]
    a[:, :, 9] = g[..., 4:]
    a[:, :, 10:] = rng.integers(4, 8, (N, 8, 6, C + G, 4)) * 2.0 ** -20
    a = (a * np.float32(2.0 ** -7)).reshape(N, 128, 4 * (C + G)).astype(BF)
    k = sg * np.exp2(np.array([-30.0, 0.0, 24.0])[o % 3])[:, None]
    u = d["u"].reshape(N, 128, 128, 4)
    u[:, :, ::16] = 0
    for h in range(8):
        z = k[:, h].astype(np.float32).astype(BF)
        u[:, 16 * h, 16 * h, 0] = z
        u[:, 16 * h + 8:16 * h + 10, 16 * h] = z[:, None, None]
    return {**d, "x": np.ascontiguousarray(a[:, :, :4 * C]), "gh": np.ascontiguousarray(a[:, :, 4 * C:]), **lists_of(rng, (), (full,)), **still(rng)}
def setup_inputs_huge(rng):
    d = numbers_of(rng)
    a = 2.0 ** 29 * (0.6 + 0.4 * rng.random((N, 128, C + G, 4)))
    c = np.stack([rng.permutation(C + G) % 2 * 2.0 - 1.0 for r in range(N)])
    one = rng.permutation(N) < N // 2
    c[one] = 1
    a = (a * c[:, None, :, None]).astype(np.float32).reshape(N, 128, 4 * (C + G)).astype(BF)
    z = 2.0 ** 30 * (1 - 0.25 * rng.random((N, 128, 8, 4))) * signs(rng)[:, None, :, None]
    d["u"].reshape(N, 128, 128, 4)[:, :, ::16] = z.astype(np.float32).astype(BF)
    return {**d, "x": np.ascontiguousarray(a[:, :, :4 * C]), "gh": np.ascontiguousarray(a[:, :, 4 * C:]), **lists_of(rng, np.flatnonzero(~one)), **still(rng)}
def setup_inputs_shapes(rng):
    e = rng.permutation(N)
    kinds = np.stack([rng.permutation(8) for r in range(N)])
    kinds[e[0]] = 2
    kinds[e[1]] = 3
    nx = np.stack([linked(rng, kinds[r, g]) for r in range(N) for g in range(8)]).reshape(N, 8, C + G)
    j = np.arange(C)
    pr = np.zeros((N, 8, R, C), int)
    for r in range(N):
        o = rng.permutation(8)
        for g in range(8):
            for t in range(R): pr[r, g, t] = (j, j ^ 1, C - 1 - j, matching(rng, C // 2))[(o[g] + t) % 4]
    return {**numbers_of(rng), **stored(nx, pr), **weights(rng, f(rng, 128, 2048))}
def setup_inputs_spread(rng):
    d = setup_inputs(rng)
    d["x"] = big(wide(rng, N, 128, 4 * C, cols=6), 1)
    d["gh"] = big(wide(rng, N, 128, 4 * G, cols=6), 1)
    return d
def check_inputs(d):
    b = []
    for k in ("x", "gh", "u", "v"):
        a = np.abs(d[k].astype(np.float32))
        if not (np.isfinite(a).all() and ((a == 0) | (a >= 2.0 ** -30) & (a <= 2.0 ** 30)).all()): b.append("a value of " + k)
    for r in range(N):
        if (np.sort(gentries(d["nx"][r]), axis=1) != np.arange(C + G)).any(): b.append("nx of rank %d is no permutation in some group" % r)
        p = gentries(d["pr"][r]).reshape(8, R, C)
        if (p < 0).any() or (p >= C).any(): b.append("pr of rank %d out of range" % r)
        elif (np.take_along_axis(p, p, axis=2) != np.arange(C)).any(): b.append("pr of rank %d: a partner's partner is another column" % r)
    if (d["wc"] != d["wc"][:1]).any(): b.append("wc differs between ranks")
    s = [mx_ref.live(p) for p in d["ws"]]
    if any((p != s[0]).any() for p in s): b.append("ws differs between ranks")
    return b
def read(X, n):
    p = np.argsort(n, axis=1)
    return (gcols(X, n[:, :C]).astype(np.float32) + gcols(X, p[:, :C]).astype(np.float32)).astype(BF)
def reference(x, gh, u, v, nx, pr, wc, ws):
    w = pk(wc[0], ws[0])
    layer = [pick(w, np.arange(128 * b, 128 * b + 128)) for b in range(4)]
    qu = [mx_ref.quantize(u[r]) for r in range(N)]
    now = [np.concatenate([x[r], gh[r]], axis=1) for r in range(N)]
    link = [gentries(nx[r]) for r in range(N)]
    pair = [gentries(pr[r]).reshape(8, R, C) for r in range(N)]
    j = np.arange(C)
    for t in range(R):
        made = []
        for r in range(N):
            q = mx_ref.quantize(read(now[r], link[r]))
            s = mx_ref.matmul(qu[r], q)[::16] + np.float32(0.0)
            a, n = pair[r][:, t], link[r][:, :C]
            o = np.take_along_axis(s, a, axis=1)
            swap = (j < a) & (s < o) | (j > a) & (o < s)
            link[r] = np.concatenate([np.where(swap, np.take_along_axis(n, a, axis=1), n), link[r][:, C:]], axis=1)
            h = tile([np.maximum(mx_ref.matmul(layer[b], q), np.float32(0.0)) * np.float32(0.015625) for b in range(4)])
            made.append(decode(mx_ref.quantize(h)).astype(BF))
        for r in range(N):
            now[r] = np.concatenate([made[r], cut(made[r ^ (1 << t % L)], 0, 4 * G)], axis=1)
    y, nl = np.zeros((N, 128, C), np.float32), np.zeros((N, 8, C + G), np.float32)
    oc, osc = np.zeros((N, 128, 4 * C), np.uint8), np.zeros((N, 16, C), np.uint8)
    for r in range(N):
        q = mx_ref.quantize(read(now[r], link[r]))
        y[r] = mx_ref.matmul(mx_ref.quantize(v[r]), q)
        nl[r] = link[r]
        oc[r], osc[r] = emit(q)
    return {"y": y, "nl": nl, "oc": oc, "osc": osc}

from concourse.mybir import dt, AluOpType, ActivationFunctionType

C, G, ROUNDS = 448, 256, 3
WC = C + G
K = WC * 4
BIG = 1048576.0
F32, BF16, I32, U16, U8, FP8 = "float32", "bfloat16", "int32", "uint16", "uint8", "float8_e4m3fn_x4"
LA, LB = "ssss", "sssv"
DA, DB, DG = "sssv", "vvss", ("sssv", "sssv", "svsv")

SCRATCH = {
    "nxi": ("sbuf", [128, 44], I32), "pri": ("sbuf", [128, 84], I32),
    "nx16": ("sbuf", [128, 44], U16), "pr16": ("sbuf", [128, 84], U16),
    "n4": ("sbuf", [128, 112], U16), "p4": ("sbuf", [128, 112], U16), "pv0": ("sbuf", [128, 28], U16),
    "wq": ("sbuf", [128, 512], FP8), "wsc": ("sbuf", [128, 512], U8),
    "ut": ("sbuf", [128, 512], BF16), "uq0": ("sbuf", [128, 128], FP8), "us0": ("sbuf", [128, 128], U8),
    "uq": ("sbuf", [128, 128], FP8), "us": ("sbuf", [128, 128], U8), "uof": ("sbuf", [128, 8], U16),
    "vt": ("sbuf", [128, 512], BF16), "vq": ("sbuf", [128, 128], FP8), "vs": ("sbuf", [128, 128], U8),
    "et": ("sbuf", [128, 2048], BF16), "eo": ("sbuf", [128, 2048], BF16),
    "eq": ("sbuf", [128, 512], FP8), "es": ("sbuf", [128, 512], U8),
    "xi": ("sbuf", [128, C], I32), "xm": ("sbuf", [128, C], I32),
    "db0": ("sbuf", [128, C], F32), "db": ("sbuf", [128, C], F32), "db2": ("sbuf", [128, C], BF16),
    "pci": ("sbuf", [128, 8], I32), "qci": ("sbuf", [128, 8], I32), "qcf": ("sbuf", [128, 8], F32),
    "colb": ("sbuf", [128, 8], F32), "col2": ("sbuf", [128, 8], F32),
    "uoi": ("sbuf", [128, 8], I32), "i84": ("sbuf", [128, 84], F32), "jw": ("sbuf", [128, 84], F32),
    "prf": ("sbuf", [128, 84], F32), "pd": ("sbuf", [128, 84], F32), "sgp": ("sbuf", [128, 84], F32), "kap": ("sbuf", [128, 84], F32),
    "iota": ("sbuf", [128, WC], F32), "sigr": ("sbuf", [128, WC], F32),
    "inv": ("sbuf", [128, WC], F32), "nxr0": ("sbuf", [128, WC], F32), "pvf": ("sbuf", [128, 28], F32),
    "sb": ("sbuf", [128, 2 * C], F32), "l16": ("sbuf", [128, 168], U16),
    "smf": ("sbuf", [128, 28], F32), "smm": ("sbuf", [128, 28], F32), "sms": ("sbuf", [128, 28], F32),
    "sig": ("sbuf", [128, 28], U16),
    "ysb": ("sbuf", [128, C], F32), "ps": ("psum", [128, 4096], F32),
}
for _t in range(4):
    SCRATCH["win%d" % _t] = ("sbuf", [128, K], BF16)
    SCRATCH["pb%d" % _t] = ("sbuf", [128, 4 * C], BF16)
    SCRATCH["z%d" % _t] = ("sbuf", [128, 4 * C], BF16)
    SCRATCH["zq%d" % _t] = ("sbuf", [128, C], FP8)
    SCRATCH["zs%d" % _t] = ("sbuf", [128, C], U8)
for _t in range(3):
    SCRATCH["h%d" % _t] = ("sbuf", [128, 4 * C], BF16)
    SCRATCH["hq%d" % _t] = ("sbuf", [128, C], FP8)
    SCRATCH["hs%d" % _t] = ("sbuf", [128, C], U8)
    SCRATCH["gq%d" % _t] = ("sbuf", [128, G], FP8)
    SCRATCH["gs%d" % _t] = ("sbuf", [128, G], U8)
    SCRATCH["nxr%d" % (_t + 1)] = ("sbuf", [128, C], F32)
    SCRATCH["pvr%d" % _t] = ("sbuf", [128, C], F32)
    SCRATCH["ssb%d" % _t] = ("sbuf", [128, C], F32)
    SCRATCH["ssc%d" % _t] = ("sbuf", [128, C], F32)
    SCRATCH["dif%d" % _t] = ("sbuf", [128, C], F32)
    SCRATCH["sgn%d" % _t] = ("sbuf", [128, C], BF16)
    SCRATCH["scd%d" % _t] = ("sbuf", [128, C], BF16)

SEMAPHORES = ["cv", "cs", "cp", "cg", "sent", "st"] + ["ld%d" % i for i in range(8)] + ["arr%d" % t for t in range(3)]


def R(name, lo, hi, step=1):
    return (name, lo, hi, step)


def rank_program(g, core, T, topo):
    rank = T.rank_of(core)
    if rank is None:
        return
    A_, F_ = AluOpType, ActivationFunctionType
    eng = {"v": g.vector, "s": g.scalar, "p": g.tensor, "g": g, "y": g.sync}
    csem = {"v": "cv", "s": "cs", "p": "cp", "g": "cg"}
    issued, waited = {}, {}
    known = {q: {} for q in eng}
    snap = {}
    log = {}

    def clash(a, lo, hi, step):
        if a[1] <= lo or hi <= a[0]: return False
        return not (a[2] == step and step > 1 and (a[0] - lo) % step)

    def region(r):
        if r[0] == "ps": return ("bank%d" % (r[1] // 512), 0, 512, 1)
        return r

    def order(q, reads, writes):
        need = {}
        for rs, wr in ((reads, False), (writes, True)):
            for r in rs:
                n, lo, hi, step = region(r)
                for a in log.get(n, []):
                    if (wr or a[3]) and clash(a, lo, hi, step):
                        s, v = a[4]
                        need[s] = max(need.get(s, 0), v)
        kn = known[q]
        todo = [(s, v) for s, v in need.items() if kn.get(s, 0) < v]
        for s, v in todo:
            if any(s2 != s and snap.get((s2, v2), {}).get(s, 0) >= v for s2, v2 in todo): continue
            eng[q].wait_ge(T.sem[s], v)
            waited[s] = max(waited.get(s, 0), v)
        for s, v in todo:
            for s2, v2 in snap.get((s, v), {}).items(): kn[s2] = max(kn.get(s2, 0), v2)
            kn[s] = max(kn.get(s, 0), v)

    def note(tok, reads, writes):
        for rs, wr in ((reads, False), (writes, True)):
            for r in rs:
                n, lo, hi, step = region(r)
                w = wr or n[:4] == "bank"
                l = log.setdefault(n, [])
                if w and step == 1: l[:] = [a for a in l if not (lo <= a[0] and a[1] <= hi)]
                l.append((lo, hi, step, w, tok))

    def run(q, reads, writes, emit, sem=None, inc=1):
        order(q, reads, writes)
        s = sem or csem[q]
        ins = emit()
        issued[s] = issued.get(s, 0) + inc
        ins.then_inc(T.sem[s], inc)
        snap[(s, issued[s])] = dict(known[q])
        note((s, issued[s]), reads, writes)

    def ap(r):
        if r[0] == "@": return ap(r[1]).indirect(ap(r[2]))
        n, lo, hi, step = r
        return T[n][:, lo:hi] if step == 1 else T[n][:, lo:hi:step]

    def ind(win, off): return ("@", win, off)

    def flat(rs):
        o = []
        for r in rs: o += [r[1], r[2]] if r[0] == "@" else [r]
        return o
    V = g.vector

    def tt(out, a, b, op): run("v", flat([a, b]), [out], lambda: V.tensor_tensor(ap(out), ap(a), ap(b), op))

    def tc(out, a):
        w = out[1] if out[0] == "@" else out
        run("v", flat([a]) + ([out[2]] if out[0] == "@" else []), [w], lambda: V.tensor_copy(ap(out), ap(a)))

    def ts(out, a, s1, s2, op0, op1=None):
        col = [s1] if isinstance(s1, tuple) else []
        v1 = ap(s1) if col else s1
        if op1 is None: run("v", [a] + col, [out], lambda: V.tensor_scalar(ap(out), ap(a), v1, None, op0))
        else: run("v", [a] + col, [out], lambda: V.tensor_scalar(ap(out), ap(a), v1, s2, op0, op1))

    def scan(out, d0, d1, op0, op1):
        run("v", [d0, d1], [out], lambda: V.tensor_tensor_scan(ap(out), ap(d0), ap(d1), 0.0, op0, op1))

    def act(out, a, fn=F_.Copy, scale=1.0, bias=0.0):
        S = g.scalar
        if isinstance(bias, tuple): run("s", flat([a, bias]), [out], lambda: S.activation(ap(out), ap(a), fn, bias=ap(bias)))
        elif scale != 1.0 and bias != 0.0: run("s", flat([a]), [out], lambda: S.activation(ap(out), ap(a), fn, bias=bias, scale=scale))
        elif scale != 1.0: run("s", flat([a]), [out], lambda: S.activation(ap(out), ap(a), fn, scale=scale))
        elif bias != 0.0: run("s", flat([a]), [out], lambda: S.activation(ap(out), ap(a), fn, bias=bias))
        else: run("s", flat([a]), [out], lambda: S.activation(ap(out), ap(a), fn))

    def copy(q, out, a):
        if q == "s": act(out, a)
        else: tc(out, a)

    def quant(q, s, t, a, b):
        run("v", [R(t, 4 * a, 4 * b)], [R(q, a, b), R(s, a, b)], lambda: V.quantize_mx(T[q][:, a:b], T[s][:, a:b], T[t][:, 4 * a:4 * b]))

    bank = [0]

    def mm(wq, ws, wa, xq, xs, a, b):
        k = bank[0] % 8
        bank[0] += 1
        o = R("ps", 512 * k, 512 * k + b - a)
        run("p", [R(wq, wa, wa + 128), R(ws, wa, wa + 128), R(xq, a, b), R(xs, a, b)], [o],
            lambda: g.tensor.matmul_mx(ap(o), T[wq][:, wa:wa + 128], T[ws][:, wa:wa + 128], T[xq][:, a:b], T[xs][:, a:b], True, True))
        return o

    def iota(name, lo, hi, pattern, base, cm):
        o = R(name, lo, hi)
        if SCRATCH[name][2] == F32: run("g", [], [o], lambda: g.iota(ap(o), pattern, base, cm, allow_small_or_imprecise_dtypes=True))
        else: run("g", [], [o], lambda: g.iota(ap(o), pattern, base, cm))

    nld = [0]

    def load(q, r, dst, src):
        s = "ld%d" % nld[0]
        nld[0] += 1
        run(q, [], [r], lambda: eng[q].dma_start(dst, src), sem=s, inc=16)

    def store(q, r, dst, src):
        run(q, [r], [], lambda: eng[q].dma_start(dst, src), sem="st", inc=16)

    load("y", R("nxi", 0, 44), T.nxi[:], T.nx[:])
    load("y", R("win0", 0, 4 * C), T.win0[:, 0:4 * C], T.x[:])
    load("y", R("win0", 4 * C, K), T.win0[:, 4 * C:K], T.gh[:])
    load("y", R("ut", 0, 512), T.ut[:], T.u[:])
    load("y", R("wq", 0, 512), T.wq[:, 0:512].bitcast(dt.uint8), T.wc[:])
    load("y", R("wsc", 0, 512), T.wsc[:], T.ws[:])
    load("y", R("pri", 0, 84), T.pri[:], T.pr[:])
    load("y", R("vt", 0, 512), T.vt[:], T.v[:])

    iota("pci", 0, 1, [[0, 1]], 0, 1)
    iota("xi", 0, C, [[0, 28], [1, 16]], 128, -1)
    iota("iota", 0, WC, [[1, WC]], 0, 0)
    iota("uoi", 0, 8, [[16, 8]], 0, 0)
    iota("i84", 0, 84, [[0, 3], [16, 28]], 0, 0)
    run("v", [], [R("et", 0, 2048)], lambda: V.memset(T.et[:], 1.0))
    run("g", [R("et", 0, 2048)], [R("eo", 0, 2048)],
        lambda: g.affine_select(T.eo[:], T.et[:], [[-1, 4], [1, 512]], A_.is_equal, 0.0, 0, -4))
    iota("sigr", C, WC, [[1, G]], C, 0)
    ts(R("qci", 0, 1), R("pci", 0, 1), 15, None, A_.bitwise_and)
    tc(R("qcf", 0, 1), R("qci", 0, 1))
    ts(R("colb", 0, 1), R("qcf", 0, 1), -BIG, 15.0 * BIG, A_.mult, A_.add)
    ts(R("xm", 0, C), R("xi", 0, C), 15, None, A_.bitwise_and)
    ts(R("db0", 0, C), R("xm", 0, C), 0.0, -32.0 * BIG, A_.is_equal, A_.mult)
    act(R("db", 0, C), R("db0", 0, C), bias=BIG)
    act(R("db2", 0, C), R("db0", 0, C), scale=2.0 / BIG, bias=2.0)
    act(R("jw", 0, 84), R("i84", 0, 84), F_.Identity, bias=R("qcf", 0, 1))
    tc(R("nx16", 0, 44), R("nxi", 0, 44))
    for e in range(4): ts(R("n4", 28 * e, 28 * e + 28), R("nxi", 0, 28), 4.0, float(e), A_.mult, A_.add)
    tc(ind(R("inv", 0, WC), R("nx16", 0, 44)), R("iota", 0, WC))
    scan(R("sb", 0, C), R("db", 0, C), R("inv", 0, C), A_.add, A_.max)
    ts(R("pvf", 0, 28), R("sb", 15, C, 16), R("colb", 0, 1), None, A_.subtract)
    for e in range(4): ts(R("p4", 28 * e, 28 * e + 28), R("pvf", 0, 28), 4.0, float(e), A_.mult, A_.add)
    act(R("nxr0", 0, WC), ind(R("iota", 0, WC), R("nx16", 0, 44)))
    store("y", R("nxr0", C, WC), T.nl[:, C:WC], T.nxr0[0:128:16, C:WC])

    def scorer():
        tc(R("pv0", 0, 28), R("pvf", 0, 28))
        tc(R("uof", 0, 8), R("uoi", 0, 8))
        quant("uq0", "us0", "ut", 0, 128)
        run("v", [R("uq0", 0, 128), R("uof", 0, 8)], [R("uq", 0, 128)],
            lambda: V.tensor_copy(T.uq[:, 0:128].bitcast(dt.uint32), T.uq0[:, 0:128].bitcast(dt.uint32).indirect(T.uof[:, 0:8])))
        run("s", [R("us0", 0, 128), R("uof", 0, 8)], [R("us", 0, 128)],
            lambda: g.scalar.activation(T.us[:, 0:128], T.us0[:, 0:128].indirect(T.uof[:, 0:8]), F_.Copy))
        tc(R("pr16", 0, 84), R("pri", 0, 84))

    def partners():
        tc(R("prf", 0, 84), R("pri", 0, 84))
        tt(R("pd", 0, 84), R("prf", 0, 84), R("jw", 0, 84), A_.subtract)
        ts(R("col2", 0, 1), R("qcf", 0, 1), -2.0, 30.0, A_.mult, A_.add)

    AB = ((0, G), (G, C))
    HALVES = ((0, C // 2), (C // 2, C))

    def windows(t, e):
        return R("win0", 0, K) if t == 0 else R("win%d" % t, WC * e, WC * e + WC)

    def offs(t, e, which, a, b):
        a, b = a // 16, b // 16
        if t == 0: return R("n4" if which == 0 else "p4", 28 * e + a, 28 * e + b)
        o = 56 * (t - 1) + 28 * which
        return R("l16", o + a, o + b)

    def fetch(t, ch):
        a, b = AB[ch]
        for e in range(4): act(R("pb%d" % t, C * e + a, C * e + b), ind(windows(t, e), offs(t, e, 0, a, b)))

    def addup(t, ch):
        a, b = AB[ch]
        for e in range(4): tt(R("z%d" % t, 4 * a + e, 4 * b, 4), ind(windows(t, e), offs(t, e, 1, a, b)), R("pb%d" % t, C * e + a, C * e + b), A_.add)
        quant("zq%d" % t, "zs%d" % t, "z%d" % t, a, b)

    def layer(t, ch):
        a, b = AB[ch]
        return [mm("wq", "wsc", 128 * k, "zq%d" % t, "zs%d" % t, a, b) for k in range(4)]

    def score(t, ch):
        a, b = AB[ch]
        return mm("uq", "us", 0, "zq%d" % t, "zs%d" % t, a, b)

    def relu(q, t, ch, k, o):
        a, b = AB[ch]
        out = R("h%d" % t, 4 * a + k, 4 * b, 4)
        if q == "s": act(out, o, F_.Relu, scale=0.015625)
        else: ts(out, o, 0.0, 0.015625, A_.max, A_.mult)

    def unpack(t, src, a, b):
        return [mm("eq", "es", 128 * k, ("gq%d" if src else "hq%d") % t, ("gs%d" if src else "hs%d") % t, a, b) for k in range(4)]

    def keep(q, t, k, o, a):
        copy(q, R("win%d" % (t + 1), WC * k + a, WC * k + a + o[2] - o[1]), o)

    def send(t):
        dst = T.cores[rank ^ (1 << t)]
        rid, pid, _ = topo.addr(dst)
        e = topo.engines(core, dst)[:8]
        m = sum(1 << i for i in e)
        h, s = "hq%d" % t, "hs%d" % t
        order("g", [R(h, 0, G), R(s, 0, G)], [])
        g.remote_dma(T["gq%d" % t][:, 0:G].bitcast(dt.uint8), T[h][:, 0:G].bitcast(dt.uint8), T.sem["arr%d" % t], T.sem.sent, pid, rid, m)
        g.remote_dma(T["gs%d" % t][:, 0:G], T[s][:, 0:G], T.sem["arr%d" % t], T.sem.sent, pid, rid, m)
        issued["sent"] = issued.get("sent", 0) + 2 * len(e)
        tok = ("arr%d" % t, 2 * len(e))
        issued[tok[0]] = tok[1]
        note(tok, [], [R("gq%d" % t, 0, G), R("gs%d" % t, 0, G)])

    for t in range(ROUNDS):
        nr = "nxr%d" % (t + 1)
        w = (28 * t, 28 * t + 28)
        ssb, ssc, dif, sgn, scd, pvr = ["%s%d" % (n, t) for n in ("ssb", "ssc", "dif", "sgn", "scd", "pvr")]
        fetch(t, 0)
        addup(t, 0)
        la = layer(t, 0)
        if t: s0 = score(t, 0)
        fetch(t, 1)
        addup(t, 1)
        if t: s1 = score(t, 1)
        for k in range(4): relu(LA[k], t, 0, k, la[k])
        quant("hq%d" % t, "hs%d" % t, "h%d" % t, 0, G)
        send(t)
        if t == 0:
            scorer()
            s0 = score(t, 0)
            s1 = score(t, 1)
            quant("eq", "es", "eo", 0, 512)
        lb = layer(t, 1)
        act(R(ssb, 0, G), s0)
        tc(R(ssc, G, C), s1)
        act(R(ssb, G, C), s1)
        tc(R(ssc, 0, G), s0)
        da = unpack(t, 0, 0, G)
        for a, b in HALVES:
            tt(R(dif, a, b), ind(R(ssb, 0, C), R("pr16", 28 * t + a // 16, 28 * t + b // 16)), R(ssc, a, b), A_.subtract)
        if t == 0: partners()
        for k in (0, 1): relu(LB[k], t, 1, k, lb[k])
        for a, b in HALVES: act(R(sgn, a, b), R(dif, a, b), F_.Sign)
        if t == 0:
            act(R("sgp", 0, 84), R("pd", 0, 84), F_.Sign)
            act(R("kap", 0, 84), R("sgp", 0, 84), F_.Identity, bias=R("col2", 0, 1))
        for k in (2, 3): relu(LB[k], t, 1, k, lb[k])
        for a, b in HALVES: scan(R(scd, a, b), R("db2", a, b), R(sgn, a, b), A_.add, A_.max)
        tt(R("smf", 0, 28), R(scd, 15, C, 16), R("kap", *w), A_.is_equal)
        tt(R("smm", 0, 28), R("smf", 0, 28), R("pd", *w), A_.mult)
        tt(R("sms", 0, 28), R("smm", 0, 28), R("jw", 0, 28), A_.add)
        tc(R("sig", 0, 28), R("sms", 0, 28))
        quant("hq%d" % t, "hs%d" % t, "h%d" % t, G, C)
        db = unpack(t, 0, G, C)
        for k in range(4):
            if DA[k] == "s": keep("s", t, k, da[k], 0)
        act(R("sigr", 0, C), ind(R("iota", 0, C), R("sig", 0, 28)))
        act(R(nr, 0, C), ind(R("nxr%d" % t, 0, C), R("sig", 0, 28)))
        for k in range(4):
            if DA[k] == "v": keep("v", t, k, da[k], 0)
        for k in range(4):
            if DB[k] == "v": keep("v", t, k, db[k], G)
        pv = R("pv0", 0, 28) if t == 0 else R("l16", 56 * t - 28, 56 * t)
        tc(R(pvr, 0, C), ind(R("sigr", 0, WC), pv))
        scan(R("sb", 0, C), R("db", 0, C), R(nr, 0, C), A_.add, A_.max)
        ts(R("l16", 56 * t, 56 * t + 28), R("sb", 15, C, 16), R("colb", 0, 1), None, A_.subtract)
        for k in range(4):
            if DB[k] == "s": keep("s", t, k, db[k], G)
        scan(R("sb", C, 2 * C), R("db", 0, C), R(pvr, 0, C), A_.add, A_.max)
        ts(R("l16", 56 * t + 28, 56 * t + 56), R("sb", C + 15, 2 * C, 16), R("colb", 0, 1), None, A_.subtract)
        if t == 2: quant("vq", "vs", "vt", 0, 128)
        dg = unpack(t, 1, 0, G)
        for k in range(4): keep(DG[t][k], t, k, dg[k], C)
    store("y", R("nxr3", 0, C), T.nl[:, 0:C], T.nxr3[0:128:16, 0:C])
    fetch(3, 0)
    addup(3, 0)
    ya = mm("vq", "vs", 0, "zq3", "zs3", 0, G)
    store("y", R("zq3", 0, G), T.oc[:, 0:4 * G], T.zq3[:, 0:G].bitcast(dt.uint8))
    fetch(3, 1)
    act(R("ysb", 0, G), ya)
    store("y", R("ysb", 0, G), T.y[:, 0:G], T.ysb[:, 0:G])
    addup(3, 1)
    yb = mm("vq", "vs", 0, "zq3", "zs3", G, C)
    for k in range(4): store("y", R("zs3", 0, C), T.osc[4 * k:4 * k + 4, 0:C], T.zs3[32 * k:32 * k + 4, 0:C])
    store("s", R("zq3", G, C), T.oc[:, 4 * G:4 * C], T.zq3[:, G:C].bitcast(dt.uint8))
    act(R("ysb", G, C), yb)
    store("s", R("ysb", G, C), T.y[:, G:C], T.ysb[:, G:C])
    for s in sorted(issued):
        if waited.get(s, 0) < issued[s]: (g if s == "sent" else g.sync).wait_ge(T.sem[s], issued[s])
